import numpy as np
import ml_dtypes


def mxq(x, axis, fmt="e4m3"):
    dtype, down = {"e4m3": (ml_dtypes.float8_e4m3fn, 7), "e5m2": (ml_dtypes.float8_e5m2, 14)}[fmt]
    v = np.moveaxis(np.asarray(x, np.float32).astype(ml_dtypes.bfloat16).astype(np.float64), axis, -1)
    blocks = v.reshape(v.shape[:-1] + (-1, 32))
    amax = np.abs(blocks).max(-1, keepdims=True)
    byte = np.maximum(np.where(amax > 0, np.frexp(amax)[1] - 1 + 127, 0) - down, 1)
    scale = np.exp2(byte - 127.0)
    codes = (blocks / scale).astype(np.float32).astype(dtype).astype(np.float64)
    return np.moveaxis((codes * scale).reshape(v.shape), -1, axis)


WIDE = False


def mx_kscale(k):
    if not WIDE:
        return np.ones(k)
    levels = np.array([10, -10, 5, -5, 0])
    if k % 512:
        return np.exp2(np.random.permutation(np.resize(levels, k // 32))).repeat(32)
    a = np.empty((k // 512, 16))
    for p in range(k // 512):
        a[p, :8] = np.random.permutation(np.resize(levels, 8))
        for g in range(8):
            far = levels[np.abs(levels - a[p, g]) >= 10]
            a[p, g + 8] = far[np.random.randint(len(far))]
    return np.exp2(a.ravel()).repeat(32)


BF16 = ml_dtypes.bfloat16


def bf(x):
    return np.asarray(x, np.float32).astype(BF16)


def f64(x):
    return np.asarray(x).astype(np.float64)


E2M1 = np.array([0.0, 0.5, 1.0, 1.5, 2.0, 3.0, 4.0, 6.0, -0.0, -0.5, -1.0, -1.5, -2.0, -3.0, -4.0, -6.0])


def pack_weight(w, fmt):
    k, n = w.shape
    w = f64(bf(w)).reshape(k // 32, 32, n)
    amax = np.abs(w).max(1)
    if fmt == "e4m3":
        byte = np.frexp(amax)[1] - 1 + 127 - 7
    else:
        mant, ex = np.frexp(amax / 6.0)
        byte = np.where(mant > 0.5, ex, ex - 1) + 127
    byte = np.clip(np.where(amax > 0, byte, 1), 1, 254)
    scaled = (w * np.exp2(127.0 - byte)[:, None, :]).reshape(k, n).astype(np.float32)
    by_word = np.ascontiguousarray(scaled.reshape(k // 512, 128, 4, n).transpose(0, 1, 3, 2))
    if fmt == "e4m3":
        words = by_word.astype(ml_dtypes.float8_e4m3fn).view(np.uint8)
    else:
        c = by_word.astype(ml_dtypes.float4_e2m1fn).view(np.uint8) & 0xF
        words = c[..., 0::2] | (c[..., 1::2] << 4)
    return np.ascontiguousarray(words), np.ascontiguousarray(byte.astype(np.uint8).reshape(k // 512, 16, n))


def unpack_weight(words, scales, fmt):
    g, p, n, _ = words.shape
    if fmt == "e4m3":
        vals = np.ascontiguousarray(words).view(ml_dtypes.float8_e4m3fn).astype(np.float64)
    else:
        nib = np.empty((g, p, n, 4), np.uint8)
        nib[..., 0::2] = words & 0xF
        nib[..., 1::2] = words >> 4
        vals = E2M1[nib]
    vals = vals * np.repeat(np.exp2(scales.astype(np.float64) - 127.0), 8, axis=1)[..., None]
    return vals.transpose(0, 1, 3, 2).reshape(g * 512, n)

E4M3FN = np.array([(-1.0 if i & 128 else 1.0) * ((1.0 + (i & 7) / 8.0) * 2.0 ** (((i >> 3) & 15) - 7) if i & 120 else (i & 7) * 2.0 ** -9) for i in range(256)])


def e4m3fn_bytes(y):
    return np.clip(np.asarray(y, np.float64), -448.0, 448.0).astype(np.float32).astype(ml_dtypes.float8_e4m3fn).view(np.uint8)


def e4m3fn_values(b):
    return E4M3FN[b]


H, W, Z, D, F, E = 32, 32, 4, 512, 512, 256


def stable_softplus(t):
    return np.maximum(t, 0.0) + np.log(1.0 + np.exp(-np.abs(t)))


def draw0():
    s, r = mx_kscale(D), mx_kscale(F)
    thw = bf(np.random.standard_normal((H, W, D)) * s)
    tzh = bf(np.random.standard_normal((Z, H, D)) * s)
    twz = bf(np.random.standard_normal((W, Z, D)) * s)
    w1_words, w1_scales = pack_weight(np.random.standard_normal((D, F)) / np.sqrt(D) / s[:, None], "e4m3")
    b1 = bf(np.random.standard_normal(F) * 0.3)
    g = bf(np.random.standard_normal(F) * r)
    w2_words, w2_scales = pack_weight(np.random.standard_normal((F, E)) / np.sqrt(F) / r[:, None], "e4m3")
    b2 = bf(np.random.standard_normal(E) * 0.3)
    return {
        "thw": thw,
        "tzh": tzh,
        "twz": twz,
        "w1_words": w1_words,
        "w1_scales": w1_scales,
        "b1": b1,
        "g": g,
        "w2_words": w2_words,
        "w2_scales": w2_scales,
        "b2": b2,
    }


def core(thw, tzh, twz, w1_words, w1_scales, b1, g, w2_words, w2_scales, b2):
    w1q = unpack_weight(w1_words, w1_scales, "e4m3")
    a = mxq(f64(thw), 2, "e4m3") @ w1q
    b = mxq(f64(tzh), 2, "e4m3") @ w1q
    c = mxq(f64(twz), 2, "e4m3") @ w1q

    a_vox = a[:, :, None, :]
    b_vox = np.transpose(b, (1, 0, 2))[:, None, :, :]
    c_vox = c[None, :, :, :]
    u = a_vox + b_vox + c_vox + f64(b1)

    v = f64(g) * stable_softplus(u)

    return (mxq(v, 3, "e4m3") @ unpack_weight(w2_words, w2_scales, "e4m3")) + f64(b2)


def setup_inputs():
    drawn = draw0()
    full = np.asarray(drawn['thw']).astype(np.float64)
    scale = (np.abs(full).reshape(32, 32, 4, 128).max(axis=(3,)) / 448.0).astype(np.float32)
    given = {}
    for key, value in drawn.items():
        if key == 'thw':
            given['thw_bytes'] = e4m3fn_bytes(full / np.repeat(scale.astype(np.float64), 128, axis=2))
            given['thw_scale'] = scale
        else:
            given[key] = value
    return given


def reference(thw_bytes, thw_scale, tzh, twz, w1_words, w1_scales, b1, g, w2_words, w2_scales, b2):
    return core(e4m3fn_values(thw_bytes) * np.repeat(thw_scale.astype(np.float64), 128, axis=2), tzh, twz, w1_words, w1_scales, b1, g, w2_words, w2_scales, b2)

@@ -1,0 +1,343 @@
+from contextlib import ExitStack
+
+import concourse.mybir as mybir
+from concourse.masks import make_identity
+
+H, W, Z, D, F, E = 32, 32, 4, 512, 512, 256
+FLOPS = 2 * (H * W + Z * H + W * Z) * D * F + 2 * H * W * Z * F * E
+
+F32 = mybir.dt.float32
+BF16 = mybir.dt.bfloat16
+I32 = mybir.dt.int32
+U32 = mybir.dt.uint32
+U8 = mybir.dt.uint8
+FP8 = mybir.dt.float8_e4m3fn
+FP8X4 = mybir.dt.float8_e4m3fn_x4
+AF = mybir.ActivationFunctionType
+ALU = mybir.AluOpType
+
+P = 128
+NU = 8
+CLIP = 32.0
+GP_SLOTS = ((0, 1, 2, 3), (0, 1, 2, 3), (0, 1), ())
+
+
+def tile_tpvformersoftplusoccupancydecoder_d1p_kernel(
+    tc, thw_bytes, thw_scale, tzh, twz, w1_words, w1_scales, b1, g, w2_words, w2_scales, b2, out
+):
+    nc = tc.nc
+    with ExitStack() as ctx:
+        keep = ctx.enter_context(tc.tile_pool(name="keep", bufs=1))
+        head = ctx.enter_context(tc.tile_pool(name="head", bufs=1))
+        grp = ctx.enter_context(tc.tile_pool(name="grp", bufs=2))
+        upool = ctx.enter_context(tc.tile_pool(name="upool", bufs=3))
+        apool = ctx.enter_context(tc.tile_pool(name="apool", bufs=3))
+        epool = ctx.enter_context(tc.tile_pool(name="epool", bufs=4))
+        vpool = ctx.enter_context(tc.tile_pool(name="vpool", bufs=3))
+        opool = ctx.enter_context(tc.tile_pool(name="opool", bufs=3))
+        ptr = ctx.enter_context(tc.psum_pool(name="ptr", bufs=2))
+        pmm = ctx.enter_context(tc.psum_pool(name="pmm", bufs=4))
+        pout = ctx.enter_context(tc.psum_pool(name="pout", bufs=2))
+        ctx.enter_context(tc.manual_schedule())
+
+        ident = keep.tile([P, P], F32)
+        byt = keep.tile([P, NU, D], U8)
+        sc0 = keep.tile([P, 4], F32)
+        sc = keep.tile([P, NU - 1, 4], F32)
+        xa = keep.tile([P, NU, D], BF16, align_bytes=64)
+        xc = keep.tile([P, D], BF16, align_bytes=64)
+        xb = keep.tile([P, D], BF16, align_bytes=64)
+        w1raw = head.tile([P, F], I32, align_bytes=64)
+        s1raw = head.tile([P, F], U8, align_bytes=64)
+        w1p = keep.tile([P, 4, P], I32, align_bytes=64)
+        s1p = keep.tile([P, 4, P], U8, align_bytes=64)
+        w2w = keep.tile([P, E], I32, align_bytes=64)
+        s2w = keep.tile([P, E], U8, align_bytes=64)
+        b1t = keep.tile([P, 4], BF16)
+        gt = keep.tile([P, 4], BF16)
+        b1f = keep.tile([P, 4], F32)
+        gq = keep.tile([P, 4], F32)
+        b2t = keep.tile([P, E], BF16)
+        cbc = keep.tile([P, 2 * P], I32, align_bytes=64)
+        cbs = keep.tile([P, 2 * P], U8, align_bytes=64)
+        crc = keep.tile([P, Z, 4, W], I32, align_bytes=64)
+        crs = keep.tile([P, Z, 4, W], U8, align_bytes=64)
+        ac = keep.tile([P, NU, P], U32, align_bytes=64)
+        as_ = keep.tile([P, NU, P], U8, align_bytes=64)
+        bp = keep.tile([P, Z, H, 4], F32)
+        dum = keep.tile([P, 1], F32)
+
+        bytes_v = thw_bytes.rearrange("(j a) w k -> (a w) j k", a=4)
+        scale_v = thw_scale.rearrange("(j a) w q -> (a w) j q", a=4)
+        nc.vector.memset(dum[:], 0.0)
+        nc.vector.memset(s1raw[:].bitcast(I32), 0)
+        nc.vector.memset(cbs[:].bitcast(I32), 0)
+        nc.vector.memset(s2w[:].bitcast(I32), 0)
+
+        nc.sync.dma_start(out=byt[:, 0, :], in_=bytes_v[:, 0, :])
+        nc.scalar.dma_start(out=sc0[:], in_=scale_v[:, 0, :])
+        nc.sync.dma_start(out=xc[:], in_=twz.rearrange("w z d -> (w z) d"))
+        nc.sync.dma_start(out=w1raw[:], in_=w1_words[0].rearrange("p n t -> p (n t)").bitcast(I32))
+        for q in range(4):
+            nc.scalar.dma_start(
+                out=s1raw[32 * q : 32 * q + 4, :].bitcast(I32),
+                in_=w1_scales[0, 4 * q : 4 * q + 4, :].bitcast(I32),
+            )
+        nc.sync.dma_start(out=xb[:], in_=tzh.rearrange("z h d -> (z h) d"))
+        nc.sync.dma_start(out=byt[:, 1, :], in_=bytes_v[:, 1, :])
+        nc.sync.dma_start(out=byt[:, 2:4, :], in_=bytes_v[:, 2:4, :])
+        nc.scalar.activation(out=dum[:], in_=dum[:], func=AF.Exp)
+        make_identity(nc, ident[:])
+        nc.gpsimd.dma_start(out=b1t[:], in_=b1.rearrange("(p t) -> p t", t=4))
+        nc.gpsimd.dma_start(out=gt[:], in_=g.rearrange("(p t) -> p t", t=4))
+        nc.sync.dma_start(out=sc[:], in_=scale_v[:, 1:, :])
+        nc.sync.dma_start(out=byt[:, 4:8, :], in_=bytes_v[:, 4:8, :])
+        nc.sync.dma_start(out=w2w[:], in_=w2_words[0].rearrange("p n t -> p (n t)").bitcast(I32))
+        for q in range(4):
+            nc.sync.dma_start(
+                out=s2w[32 * q : 32 * q + 4, :].bitcast(I32),
+                in_=w2_scales[0, 4 * q : 4 * q + 4, :].bitcast(I32),
+            )
+        nc.sync.dma_start(out=b2t[:], in_=b2.partition_broadcast(P))
+
+        def widen(j, q, vec):
+            cols = slice(128 * q, 128 * q + 128)
+            src = byt[:, j, cols].bitcast(FP8)
+            s = sc0[:, q : q + 1] if j == 0 else sc[:, j - 1, q : q + 1]
+            if vec:
+                nc.vector.tensor_scalar(out=xa[:, j, cols], in0=src, scalar1=s, scalar2=None, op0=ALU.mult)
+            else:
+                nc.scalar.activation(out=xa[:, j, cols], in_=src, func=AF.Copy, scale=s)
+
+        def turn(dst, src):
+            words = src.bitcast(F32)
+            for u in range(2):
+                nc.tensor.transpose(dst[:, u, :], words[:, u : 2 * P : 2], ident[:])
+
+        banks = {}
+
+        def turn_a(first, count):
+            bank = ptr.tile([P, 2, 2, P], F32, name="trb")
+            for s in range(count):
+                turn(bank[:, s], xa[:, first + s, :])
+            banks["a"] = bank
+
+        def copy_a(count):
+            ga = grp.tile([P, 2, P, 4], BF16, name="ga", align_bytes=64)
+            nc.scalar.copy(
+                out=ga[:, 0:count].rearrange("p s r e -> p (s r e)").bitcast(F32).rearrange("p (s r u) -> p s r u", s=count, u=2),
+                in_=banks["a"][:, 0:count].rearrange("p s u r -> p s r u"),
+            )
+            return ga
+
+        def quant_a(ga, first, count):
+            nc.vector.quantize_mx(
+                out=ac[:, first : first + count, :].rearrange("p s r -> p (s r)").bitcast(FP8X4),
+                scales=as_[:, first : first + count, :].rearrange("p s r -> p (s r)"),
+                in_=ga[:, 0:count].rearrange("p s r e -> p (s r e)"),
+            )
+
+        def project(j, z):
+            bank = pmm.tile([P, 4, P], F32, name="mmb")
+            for t in range(4):
+                nc.tensor.matmul_mx(
+                    out=bank[:, t, :],
+                    lhsT=w1p[:, t, :].bitcast(FP8X4), lhsT_scale=s1p[:, t, :],
+                    rhs=ac[:, j, :].bitcast(FP8X4), rhs_scale=as_[:, j, :],
+                    start=True, stop=False,
+                )
+                nc.tensor.matmul_mx(
+                    out=bank[:, t, :],
+                    lhsT=w1p[:, t, :].bitcast(FP8X4), lhsT_scale=s1p[:, t, :],
+                    rhs=crc[:, z].rearrange("p a w -> p (a w)").bitcast(FP8X4),
+                    rhs_scale=crs[:, z].rearrange("p a w -> p (a w)"),
+                    start=False, stop=True,
+                )
+            return bank
+
+        us, es, as_pairs = {}, {}, {}
+
+        def add_b(j, z, bank):
+            pair, s = divmod(j, 2)
+            if s == 0 and z == 0:
+                us[pair] = upool.tile([P, 2, 512, 4], F32, name="ut")
+            nc.vector.tensor_tensor(
+                out=us[pair][:, s, 128 * z : 128 * z + 128, :].rearrange("p (a w) t -> p a w t", a=4),
+                in0=bank[:].rearrange("p t (a w) -> p a w t", a=4),
+                in1=bp[:, z, 4 * j : 4 * j + 4, :].unsqueeze(2).to_broadcast([P, 4, W, 4]),
+                op=ALU.add,
+            )
+
+        def expo(j, half):
+            pair, s = divmod(j, 2)
+            if s == 0 and half == 0:
+                es[pair] = epool.tile([P, 2, 2048], F32, name="et")
+            nc.scalar.activation(
+                out=es[pair][:, s, 1024 * half : 1024 * half + 1024],
+                in_=us[pair][:, s, 256 * half : 256 * half + 256, :].rearrange("p n t -> p (n t)"),
+                func=AF.Exp,
+            )
+
+        def loga(j):
+            pair, s = divmod(j, 2)
+            e = es[pair][:, s, :]
+            nc.scalar.activation(out=e, in_=e, func=AF.Ln, bias=1.0)
+
+        def guard(pair, t, eng):
+            if pair not in as_pairs:
+                as_pairs[pair] = apool.tile([P, 4, 1024], F32, name="at")
+            eng.tensor_scalar(
+                out=as_pairs[pair][:, t, :],
+                in0=us[pair][:].rearrange("p s n t -> p t (s n)")[:, t, :],
+                scalar1=CLIP, scalar2=gq[:, t : t + 1], op0=ALU.max, op1=ALU.mult,
+            )
+
+        vts, vqs, obs = {}, {}, {}
+
+        def combine(j):
+            pair, s = divmod(j, 2)
+            vt = vpool.tile([P, 512, 4], BF16, name="vt", align_bytes=64)
+            nc.vector.scalar_tensor_tensor(
+                out=vt[:],
+                in0=es[pair][:, s, :].rearrange("p (n t) -> p n t", t=4),
+                scalar=CLIP,
+                in1=as_pairs[pair][:, :, 512 * s : 512 * s + 512].rearrange("p t n -> p n t"),
+                op0=ALU.min, op1=ALU.mult,
+            )
+            vts[j] = vt
+
+        def quant_v(j):
+            vc = vpool.tile([P, 512], U32, name="vc", align_bytes=64)
+            vs = vpool.tile([P, 512], U8, name="vs", align_bytes=64)
+            nc.vector.quantize_mx(
+                out=vc[:].bitcast(FP8X4), scales=vs[:], in_=vts[j][:].rearrange("p n t -> p (n t)")
+            )
+            vqs[j] = (vc, vs)
+
+        def decode(j):
+            vc, vs = vqs[j]
+            for zp in range(2):
+                ob = pout.tile([P, 2, E], F32, name="ob")
+                for zz in range(2):
+                    cols = slice(128 * (2 * zp + zz), 128 * (2 * zp + zz) + 128)
+                    nc.tensor.matmul_mx(
+                        out=ob[:, zz, :],
+                        lhsT=vc[:, cols].bitcast(FP8X4), lhsT_scale=vs[:, cols],
+                        rhs=w2w[:].bitcast(FP8X4), rhs_scale=s2w[:],
+                        start=True, stop=True,
+                    )
+                obs[j, zp] = ob
+
+        out_v = out.rearrange("(j a) w z e -> (a w) j z e", a=4)
+
+        def finish(j):
+            ot = opool.tile([P, Z, E], F32, name="ot")
+            for zp in range(2):
+                nc.vector.tensor_tensor(
+                    out=ot[:, 2 * zp : 2 * zp + 2, :], in0=obs[j, zp][:],
+                    in1=b2t[:].unsqueeze(1).to_broadcast([P, 2, E]), op=ALU.add,
+                )
+                if j == NU - 1:
+                    nc.sync.dma_start(out=out_v[:, j, 2 * zp : 2 * zp + 2, :], in_=ot[:, 2 * zp : 2 * zp + 2, :])
+            if j < NU - 1:
+                nc.sync.dma_start(out=out_v[:, j], in_=ot[:])
+
+        widen(0, 0, True)
+        widen(0, 2, False)
+        widen(0, 1, True)
+        widen(0, 3, False)
+        cb = ptr.tile([P, 2, 2, P], F32, name="trb")
+        turn(cb[:, 0], xc[:])
+        turn(cb[:, 1], xb[:])
+        turn_a(0, 1)
+        gcb = grp.tile([P, 2, P, 4], BF16, name="gcb", align_bytes=64)
+        gw = gcb[:].rearrange("p s r e -> p (s r e)").bitcast(F32)
+        nc.vector.tensor_copy(
+            out=gw[:, 0:256].rearrange("p (z w u) -> p z w u", z=Z, u=2),
+            in_=cb[:, 0].rearrange("p u (w z) -> p z w u", z=Z),
+        )
+        nc.scalar.copy(
+            out=gw[:, 256:512].rearrange("p (r u) -> p r u", u=2),
+            in_=cb[:, 1].rearrange("p u r -> p r u"),
+        )
+        ga0 = copy_a(1)
+        for q in range(4):
+            widen(1, q, False)
+        nc.vector.tensor_copy(out=w1p[:], in_=w1raw[:].rearrange("p (m t) -> p t m", t=4))
+        nc.vector.tensor_copy(out=s1p[:], in_=s1raw[:].rearrange("p (m t) -> p t m", t=4))
+        nc.vector.quantize_mx(
+            out=cbc[:].bitcast(FP8X4), scales=cbs[:], in_=gcb[:].rearrange("p s r e -> p (s r e)")
+        )
+        nc.vector.tensor_copy(
+            out=crc[:], in_=cbc[:, 0:P].rearrange("p (z w) -> p z w", z=Z).unsqueeze(2).to_broadcast([P, Z, 4, W])
+        )
+        nc.vector.tensor_copy(
+            out=crs[:].rearrange("p z a w -> p (z a w)").bitcast(I32).rearrange("p (z a w) -> p z a w", z=Z, a=4),
+            in_=cbs[:, 0:P].bitcast(I32).rearrange("p (z w) -> p z w", z=Z).unsqueeze(2).to_broadcast([P, Z, 4, W // 4]),
+        )
+        quant_a(ga0, 0, 1)
+        nc.vector.tensor_copy(out=b1f[:], in_=b1t[:])
+        nc.vector.tensor_scalar(out=gq[:], in0=gt[:], scalar1=1.0 / CLIP, scalar2=None, op0=ALU.mult)
+        bb = pmm.tile([P, 4, P], F32, name="mmb")
+        for t in range(4):
+            nc.tensor.matmul_mx(
+                out=bb[:, t, :],
+                lhsT=w1p[:, t, :].bitcast(FP8X4), lhsT_scale=s1p[:, t, :],
+                rhs=cbc[:, P : 2 * P].bitcast(FP8X4), rhs_scale=cbs[:, P : 2 * P],
+                start=True, stop=True,
+            )
+        nc.vector.tensor_tensor(
+            out=bp[:].rearrange("p z h t -> p (z h) t"), in0=bb[:].rearrange("p t r -> p r t"),
+            in1=b1f[:].unsqueeze(1).to_broadcast([P, P, 4]), op=ALU.add,
+        )
+        turn_a(1, 1)
+        ga = copy_a(1)
+        for j in (2, 3):
+            for q in range(4):
+                widen(j, q, False)
+
+        for j in range(NU):
+            if j == 0:
+                quant_a(ga, 1, 1)
+            for z in range(Z):
+                bank = project(j, z)
+                add_b(j, z, bank)
+                if j < 4 and z % 2 == 1:
+                    expo(j, z // 2)
+            if j < 3:
+                first = 2 * j + 2
+                turn_a(first, 2)
+                ga = copy_a(2)
+                quant_a(ga, first, 2)
+                if j < 2:
+                    for jj in (first + 2, first + 3):
+                        for q in range(4):
+                            widen(jj, q, False)
+            if j % 2 == 1:
+                for t in range(4):
+                    if t in GP_SLOTS[j // 2]:
+                        guard(j // 2, t, nc.gpsimd)
+        for j in range(4):
+            loga(j)
+        for j in range(4, NU):
+            for half in range(2):
+                expo(j, half)
+        for j in range(4, NU):
+            loga(j)
+
+        def guard_vec(pair):
+            for t in range(4):
+                if t not in GP_SLOTS[pair]:
+                    guard(pair, t, nc.vector)
+
+        guard_vec(2)
+        for k in range(NU + 2):
+            if k < NU:
+                combine(k)
+            if k == 1:
+                guard_vec(3)
+            if 1 <= k <= NU:
+                quant_v(k - 1)
+                decode(k - 1)
+            if k >= 2:
+                finish(k - 2)

@@ -1,3 +1,4 @@
+import math
 from contextlib import ExitStack
 
 import concourse.mybir as mybir
@@ -19,7 +20,7 @@ ALU = mybir.AluOpType
 P = 128
 NU = 8
 CLIP = 32.0
-GP_SLOTS = ((0, 1, 2, 3), (0, 1, 2, 3), (0, 1), ())
+ECLIP = math.exp(CLIP)
 
 
 def tile_tpvformersoftplusoccupancydecoder_d1p_kernel(
@@ -30,9 +31,8 @@ def tile_tpvformersoftplusoccupancydecoder_d1p_kernel(
         keep = ctx.enter_context(tc.tile_pool(name="keep", bufs=1))
         head = ctx.enter_context(tc.tile_pool(name="head", bufs=1))
         grp = ctx.enter_context(tc.tile_pool(name="grp", bufs=2))
-        upool = ctx.enter_context(tc.tile_pool(name="upool", bufs=3))
-        apool = ctx.enter_context(tc.tile_pool(name="apool", bufs=3))
-        epool = ctx.enter_context(tc.tile_pool(name="epool", bufs=4))
+        upool = ctx.enter_context(tc.tile_pool(name="upool", bufs=4))
+        epool = ctx.enter_context(tc.tile_pool(name="epool", bufs=8))
         vpool = ctx.enter_context(tc.tile_pool(name="vpool", bufs=3))
         opool = ctx.enter_context(tc.tile_pool(name="opool", bufs=3))
         ptr = ctx.enter_context(tc.psum_pool(name="ptr", bufs=2))
@@ -64,7 +64,7 @@ def tile_tpvformersoftplusoccupancydecoder_d1p_kernel(
         crs = keep.tile([P, Z, 4, W], U8, align_bytes=64)
         ac = keep.tile([P, NU, P], U32, align_bytes=64)
         as_ = keep.tile([P, NU, P], U8, align_bytes=64)
-        bp = keep.tile([P, Z, H, 4], F32)
+        bp = keep.tile([P, 4, Z, H], F32)
         dum = keep.tile([P, 1], F32)
 
         bytes_v = thw_bytes.rearrange("(j a) w k -> (a w) j k", a=4)
@@ -155,54 +155,51 @@ def tile_tpvformersoftplusoccupancydecoder_d1p_kernel(
                 )
             return bank
 
-        us, es, as_pairs = {}, {}, {}
+        us, es = {}, {}
 
         def add_b(j, z, bank):
             pair, s = divmod(j, 2)
             if s == 0 and z == 0:
-                us[pair] = upool.tile([P, 2, 512, 4], F32, name="ut")
+                us[pair] = upool.tile([P, 4, 2, 512], F32, name="ut")
             nc.vector.tensor_tensor(
-                out=us[pair][:, s, 128 * z : 128 * z + 128, :].rearrange("p (a w) t -> p a w t", a=4),
-                in0=bank[:].rearrange("p t (a w) -> p a w t", a=4),
-                in1=bp[:, z, 4 * j : 4 * j + 4, :].unsqueeze(2).to_broadcast([P, 4, W, 4]),
+                out=us[pair][:, :, s, 128 * z : 128 * z + 128].rearrange("p t (a w) -> p t a w", a=4),
+                in0=bank[:].rearrange("p t (a w) -> p t a w", a=4),
+                in1=bp[:, :, z, 4 * j : 4 * j + 4].unsqueeze(3).to_broadcast([P, 4, 4, W]),
                 op=ALU.add,
             )
 
         def expo(j, half):
             pair, s = divmod(j, 2)
-            if s == 0 and half == 0:
-                es[pair] = epool.tile([P, 2, 2048], F32, name="et")
-            nc.scalar.activation(
-                out=es[pair][:, s, 1024 * half : 1024 * half + 1024],
-                in_=us[pair][:, s, 256 * half : 256 * half + 256, :].rearrange("p n t -> p (n t)"),
-                func=AF.Exp,
-            )
+            if half == 0:
+                es[j] = epool.tile([P, 4, 512], F32, name="et")
+            cols = slice(256 * half, 256 * half + 256)
+            nc.scalar.activation(out=es[j][:, :, cols], in_=us[pair][:, :, s, cols], func=AF.Exp)
+
+        def clip(j):
+            e = es[j][:].rearrange("p t n -> p (t n)")
+            nc.gpsimd.tensor_scalar(out=e, in0=e, scalar1=ECLIP, scalar2=1.0, op0=ALU.min, op1=ALU.mult)
 
         def loga(j):
-            pair, s = divmod(j, 2)
-            e = es[pair][:, s, :]
+            e = es[j][:].rearrange("p t n -> p (t n)")
             nc.scalar.activation(out=e, in_=e, func=AF.Ln, bias=1.0)
 
-        def guard(pair, t, eng):
-            if pair not in as_pairs:
-                as_pairs[pair] = apool.tile([P, 4, 1024], F32, name="at")
-            eng.tensor_scalar(
-                out=as_pairs[pair][:, t, :],
-                in0=us[pair][:].rearrange("p s n t -> p t (s n)")[:, t, :],
-                scalar1=CLIP, scalar2=gq[:, t : t + 1], op0=ALU.max, op1=ALU.mult,
-            )
+        def guard(pair):
+            for t in range(4):
+                a = us[pair][:, t].rearrange("p s n -> p (s n)")
+                nc.vector.tensor_scalar(
+                    out=a, in0=a, scalar1=CLIP, scalar2=gq[:, t : t + 1], op0=ALU.max, op1=ALU.mult
+                )
 
         vts, vqs, obs = {}, {}, {}
 
         def combine(j):
             pair, s = divmod(j, 2)
             vt = vpool.tile([P, 512, 4], BF16, name="vt", align_bytes=64)
-            nc.vector.scalar_tensor_tensor(
-                out=vt[:],
-                in0=es[pair][:, s, :].rearrange("p (n t) -> p n t", t=4),
-                scalar=CLIP,
-                in1=as_pairs[pair][:, :, 512 * s : 512 * s + 512].rearrange("p t n -> p n t"),
-                op0=ALU.min, op1=ALU.mult,
+            nc.vector.tensor_tensor(
+                out=vt[:].rearrange("p (c i) t -> p c t i", i=4),
+                in0=es[j][:].rearrange("p t (c i) -> p c t i", i=4),
+                in1=us[pair][:, :, s, :].rearrange("p t (c i) -> p c t i", i=4),
+                op=ALU.mult,
             )
             vts[j] = vt
 
@@ -287,8 +284,8 @@ def tile_tpvformersoftplusoccupancydecoder_d1p_kernel(
                 start=True, stop=True,
             )
         nc.vector.tensor_tensor(
-            out=bp[:].rearrange("p z h t -> p (z h) t"), in0=bb[:].rearrange("p t r -> p r t"),
-            in1=b1f[:].unsqueeze(1).to_broadcast([P, P, 4]), op=ALU.add,
+            out=bp[:].rearrange("p t z h -> p t (z h)"), in0=bb[:],
+            in1=b1f[:].unsqueeze(2).to_broadcast([P, 4, P]), op=ALU.add,
         )
         turn_a(1, 1)
         ga = copy_a(1)
@@ -302,8 +299,9 @@ def tile_tpvformersoftplusoccupancydecoder_d1p_kernel(
             for z in range(Z):
                 bank = project(j, z)
                 add_b(j, z, bank)
-                if j < 4 and z % 2 == 1:
+                if z % 2 == 1:
                     expo(j, z // 2)
+            clip(j)
             if j < 3:
                 first = 2 * j + 2
                 turn_a(first, 2)
@@ -313,29 +311,16 @@ def tile_tpvformersoftplusoccupancydecoder_d1p_kernel(
                     for jj in (first + 2, first + 3):
                         for q in range(4):
                             widen(jj, q, False)
-            if j % 2 == 1:
-                for t in range(4):
-                    if t in GP_SLOTS[j // 2]:
-                        guard(j // 2, t, nc.gpsimd)
-        for j in range(4):
-            loga(j)
-        for j in range(4, NU):
-            for half in range(2):
-                expo(j, half)
-        for j in range(4, NU):
+            if j in (3, 5, 7):
+                guard(j // 2 - 1)
+        for j in range(NU):
             loga(j)
 
-        def guard_vec(pair):
-            for t in range(4):
-                if t not in GP_SLOTS[pair]:
-                    guard(pair, t, nc.vector)
-
-        guard_vec(2)
         for k in range(NU + 2):
             if k < NU:
                 combine(k)
-            if k == 1:
-                guard_vec(3)
+            if k == 0:
+                guard(3)
             if 1 <= k <= NU:
                 quant_v(k - 1)
                 decode(k - 1)

@@ -31,7 +31,8 @@ def tile_tpvformersoftplusoccupancydecoder_d1p_kernel(
         keep = ctx.enter_context(tc.tile_pool(name="keep", bufs=1))
         head = ctx.enter_context(tc.tile_pool(name="head", bufs=1))
         grp = ctx.enter_context(tc.tile_pool(name="grp", bufs=2))
-        upool = ctx.enter_context(tc.tile_pool(name="upool", bufs=4))
+        upool = ctx.enter_context(tc.tile_pool(name="upool", bufs=2))
+        apool = ctx.enter_context(tc.tile_pool(name="apool", bufs=4))
         epool = ctx.enter_context(tc.tile_pool(name="epool", bufs=8))
         vpool = ctx.enter_context(tc.tile_pool(name="vpool", bufs=3))
         opool = ctx.enter_context(tc.tile_pool(name="opool", bufs=3))
@@ -60,8 +61,13 @@ def tile_tpvformersoftplusoccupancydecoder_d1p_kernel(
         b2t = keep.tile([P, E], BF16)
         cbc = keep.tile([P, 2 * P], I32, align_bytes=64)
         cbs = keep.tile([P, 2 * P], U8, align_bytes=64)
-        crc = keep.tile([P, Z, 4, W], I32, align_bytes=64)
-        crs = keep.tile([P, Z, 4, W], U8, align_bytes=64)
+        crc = keep.tile([P, Z, 16, W], I32, align_bytes=64)
+        crs = keep.tile([P, Z, 16, W], U8, align_bytes=64)
+        brc = keep.tile([P, Z, 16, W], I32, align_bytes=64)
+        brs = keep.tile([P, Z, 16, W], U8, align_bytes=64)
+        bsq = keep.tile([P, Z, 16, 4], U8, align_bytes=64)
+        gf = keep.tile([P, 4], F32)
+        b1c = keep.tile([P, 4], F32)
         ac = keep.tile([P, NU, P], U32, align_bytes=64)
         as_ = keep.tile([P, NU, P], U8, align_bytes=64)
         bp = keep.tile([P, 4, Z, H], F32)
@@ -74,23 +80,28 @@ def tile_tpvformersoftplusoccupancydecoder_d1p_kernel(
         nc.vector.memset(cbs[:].bitcast(I32), 0)
         nc.vector.memset(s2w[:].bitcast(I32), 0)
 
-        nc.sync.dma_start(out=byt[:, 0, :], in_=bytes_v[:, 0, :])
-        nc.scalar.dma_start(out=sc0[:], in_=scale_v[:, 0, :])
-        nc.sync.dma_start(out=xc[:], in_=twz.rearrange("w z d -> (w z) d"))
-        nc.sync.dma_start(out=w1raw[:], in_=w1_words[0].rearrange("p n t -> p (n t)").bitcast(I32))
-        for q in range(4):
-            nc.scalar.dma_start(
+        def load_s1(q, eng):
+            eng.dma_start(
                 out=s1raw[32 * q : 32 * q + 4, :].bitcast(I32),
                 in_=w1_scales[0, 4 * q : 4 * q + 4, :].bitcast(I32),
             )
+
+        nc.sync.dma_start(out=byt[:, 0, :], in_=bytes_v[:, 0, :])
+        nc.scalar.dma_start(out=sc0[:], in_=scale_v[:, 0, :])
+        nc.sync.dma_start(out=xc[:], in_=twz.rearrange("w z d -> (w z) d"))
+        nc.scalar.dma_start(out=w1raw[:], in_=w1_words[0].rearrange("p n t -> p (n t)").bitcast(I32))
         nc.sync.dma_start(out=xb[:], in_=tzh.rearrange("z h d -> (z h) d"))
-        nc.sync.dma_start(out=byt[:, 1, :], in_=bytes_v[:, 1, :])
-        nc.sync.dma_start(out=byt[:, 2:4, :], in_=bytes_v[:, 2:4, :])
+        load_s1(0, nc.scalar)
+        load_s1(1, nc.scalar)
+        load_s1(2, nc.sync)
+        load_s1(3, nc.sync)
         nc.scalar.activation(out=dum[:], in_=dum[:], func=AF.Exp)
-        make_identity(nc, ident[:])
-        nc.gpsimd.dma_start(out=b1t[:], in_=b1.rearrange("(p t) -> p t", t=4))
-        nc.gpsimd.dma_start(out=gt[:], in_=g.rearrange("(p t) -> p t", t=4))
+        nc.sync.dma_start(out=b1t[:], in_=b1.rearrange("(p t) -> p t", t=4))
+        nc.sync.dma_start(out=byt[:, 1, :], in_=bytes_v[:, 1, :])
         nc.sync.dma_start(out=sc[:], in_=scale_v[:, 1:, :])
+        nc.sync.dma_start(out=byt[:, 2:4, :], in_=bytes_v[:, 2:4, :])
+        make_identity(nc, ident[:])
+        nc.gpsimd.dma_start(out=gt[:], in_=g.rearrange("(p t) -> p t", t=4))
         nc.sync.dma_start(out=byt[:, 4:8, :], in_=bytes_v[:, 4:8, :])
         nc.sync.dma_start(out=w2w[:], in_=w2_words[0].rearrange("p n t -> p (n t)").bitcast(I32))
         for q in range(4):
@@ -99,6 +110,10 @@ def tile_tpvformersoftplusoccupancydecoder_d1p_kernel(
                 in_=w2_scales[0, 4 * q : 4 * q + 4, :].bitcast(I32),
             )
         nc.sync.dma_start(out=b2t[:], in_=b2.partition_broadcast(P))
+        nc.gpsimd.tensor_copy(out=b1f[:], in_=b1t[:])
+        nc.gpsimd.tensor_scalar(out=gq[:], in0=gt[:], scalar1=1.0 / CLIP, scalar2=0.0, op0=ALU.mult, op1=ALU.add)
+        nc.gpsimd.tensor_copy(out=gf[:], in_=gt[:])
+        nc.gpsimd.tensor_scalar(out=b1c[:], in0=b1t[:], scalar1=1.0, scalar2=-CLIP, op0=ALU.mult, op1=ALU.add)
 
         def widen(j, q, vec):
             cols = slice(128 * q, 128 * q + 128)
@@ -149,8 +164,8 @@ def tile_tpvformersoftplusoccupancydecoder_d1p_kernel(
                 nc.tensor.matmul_mx(
                     out=bank[:, t, :],
                     lhsT=w1p[:, t, :].bitcast(FP8X4), lhsT_scale=s1p[:, t, :],
-                    rhs=crc[:, z].rearrange("p a w -> p (a w)").bitcast(FP8X4),
-                    rhs_scale=crs[:, z].rearrange("p a w -> p (a w)"),
+                    rhs=crc[:, z, 0:4].rearrange("p a w -> p (a w)").bitcast(FP8X4),
+                    rhs_scale=crs[:, z, 0:4].rearrange("p a w -> p (a w)"),
                     start=False, stop=True,
                 )
             return bank
@@ -177,7 +192,7 @@ def tile_tpvformersoftplusoccupancydecoder_d1p_kernel(
 
         def clip(j):
             e = es[j][:].rearrange("p t n -> p (t n)")
-            nc.gpsimd.tensor_scalar(out=e, in0=e, scalar1=ECLIP, scalar2=1.0, op0=ALU.min, op1=ALU.mult)
+            nc.vector.tensor_scalar(out=e, in0=e, scalar1=ECLIP, scalar2=None, op0=ALU.min)
 
         def loga(j):
             e = es[j][:].rearrange("p t n -> p (t n)")
@@ -190,15 +205,58 @@ def tile_tpvformersoftplusoccupancydecoder_d1p_kernel(
                     out=a, in0=a, scalar1=CLIP, scalar2=gq[:, t : t + 1], op0=ALU.max, op1=ALU.mult
                 )
 
+        ybanks, ya = {}, {}
+
+        def y_project(z):
+            for t in range(4):
+                bank = pmm.tile([P, 512], F32, name="mmb")
+                for i, (codes, scales) in enumerate((
+                    (ac[:, 4:8].rearrange("p j r -> p (j r)"), as_[:, 4:8].rearrange("p j r -> p (j r)")),
+                    (crc[:, z].rearrange("p a w -> p (a w)"), crs[:, z].rearrange("p a w -> p (a w)")),
+                    (brc[:, z].rearrange("p a w -> p (a w)"), brs[:, z].rearrange("p a w -> p (a w)")),
+                )):
+                    nc.tensor.matmul_mx(
+                        out=bank[:],
+                        lhsT=w1p[:, t, :].bitcast(FP8X4), lhsT_scale=s1p[:, t, :],
+                        rhs=codes.bitcast(FP8X4), rhs_scale=scales,
+                        start=i == 0, stop=i == 2,
+                    )
+                ybanks[z, t] = bank
+
+        def y_evacuate(z, excess=True):
+            es[4 + z] = epool.tile([P, 4, 512], F32, name="et")
+            ya[z] = apool.tile([P, 4, 512], F32, name="yt")
+            for t in range(4):
+                bank = ybanks[z, t]
+                nc.scalar.activation(out=es[4 + z][:, t, :], in_=bank[:], func=AF.Exp, bias=b1f[:, t : t + 1])
+                if not excess:
+                    continue
+                nc.scalar.activation(out=ya[z][:, t, :], in_=bank[:], func=AF.Relu, bias=b1c[:, t : t + 1])
+                nc.gpsimd.tensor_scalar(
+                    out=ya[z][:, t, :], in0=ya[z][:, t, :],
+                    scalar1=gq[:, t : t + 1], scalar2=gf[:, t : t + 1], op0=ALU.mult, op1=ALU.add,
+                )
+
+        def y_excess(z):
+            for t in range(4):
+                nc.vector.tensor_scalar(
+                    out=ya[z][:, t, :], in0=ybanks[z, t][:], scalar1=b1c[:, t : t + 1], scalar2=0.0,
+                    op0=ALU.add, op1=ALU.max,
+                )
+                nc.gpsimd.tensor_scalar(
+                    out=ya[z][:, t, :], in0=ya[z][:, t, :],
+                    scalar1=gq[:, t : t + 1], scalar2=gf[:, t : t + 1], op0=ALU.mult, op1=ALU.add,
+                )
+
         vts, vqs, obs = {}, {}, {}
 
         def combine(j):
-            pair, s = divmod(j, 2)
+            a = us[j // 2][:, :, j % 2, :] if j < 4 else ya[j - 4][:]
             vt = vpool.tile([P, 512, 4], BF16, name="vt", align_bytes=64)
             nc.vector.tensor_tensor(
                 out=vt[:].rearrange("p (c i) t -> p c t i", i=4),
                 in0=es[j][:].rearrange("p t (c i) -> p c t i", i=4),
-                in1=us[pair][:, :, s, :].rearrange("p t (c i) -> p c t i", i=4),
+                in1=a.rearrange("p t (c i) -> p c t i", i=4),
                 op=ALU.mult,
             )
             vts[j] = vt
@@ -228,53 +286,71 @@ def tile_tpvformersoftplusoccupancydecoder_d1p_kernel(
         out_v = out.rearrange("(j a) w z e -> (a w) j z e", a=4)
 
         def finish(j):
-            ot = opool.tile([P, Z, E], F32, name="ot")
+            ot = opool.tile([P, 4, E], F32, name="ot")
+            dst = out_v[:, j] if j < 4 else out_v[:, 4:8, j - 4, :]
             for zp in range(2):
                 nc.vector.tensor_tensor(
                     out=ot[:, 2 * zp : 2 * zp + 2, :], in0=obs[j, zp][:],
                     in1=b2t[:].unsqueeze(1).to_broadcast([P, 2, E]), op=ALU.add,
                 )
                 if j == NU - 1:
-                    nc.sync.dma_start(out=out_v[:, j, 2 * zp : 2 * zp + 2, :], in_=ot[:, 2 * zp : 2 * zp + 2, :])
+                    nc.sync.dma_start(out=dst[:, 2 * zp : 2 * zp + 2], in_=ot[:, 2 * zp : 2 * zp + 2, :])
             if j < NU - 1:
-                nc.sync.dma_start(out=out_v[:, j], in_=ot[:])
+                nc.sync.dma_start(out=dst, in_=ot[:])
 
-        widen(0, 0, True)
-        widen(0, 2, False)
-        widen(0, 1, True)
-        widen(0, 3, False)
-        cb = ptr.tile([P, 2, 2, P], F32, name="trb")
-        turn(cb[:, 0], xc[:])
-        turn(cb[:, 1], xb[:])
-        turn_a(0, 1)
-        gcb = grp.tile([P, 2, P, 4], BF16, name="gcb", align_bytes=64)
-        gw = gcb[:].rearrange("p s r e -> p (s r e)").bitcast(F32)
+        for q in range(4):
+            widen(0, q, True)
+        cbank = ptr.tile([P, 2, 2, P], F32, name="trb")
+        turn(cbank[:, 0], xc[:])
+        gc = grp.tile([P, P, 4], BF16, name="gc", align_bytes=64)
         nc.vector.tensor_copy(
-            out=gw[:, 0:256].rearrange("p (z w u) -> p z w u", z=Z, u=2),
-            in_=cb[:, 0].rearrange("p u (w z) -> p z w u", z=Z),
+            out=gc[:].rearrange("p r e -> p (r e)").bitcast(F32).rearrange("p (z w u) -> p z w u", z=Z, u=2),
+            in_=cbank[:, 0].rearrange("p u (w z) -> p z w u", z=Z),
         )
-        nc.scalar.copy(
-            out=gw[:, 256:512].rearrange("p (r u) -> p r u", u=2),
-            in_=cb[:, 1].rearrange("p u r -> p r u"),
-        )
+        turn_a(0, 1)
         ga0 = copy_a(1)
+        bbank = ptr.tile([P, 2, 2, P], F32, name="trb")
+        turn(bbank[:, 0], xb[:])
+        gb = grp.tile([P, P, 4], BF16, name="gb", align_bytes=64)
+        nc.scalar.copy(
+            out=gb[:].rearrange("p r e -> p (r e)").bitcast(F32).rearrange("p (r u) -> p r u", u=2),
+            in_=bbank[:, 0].rearrange("p u r -> p r u"),
+        )
+        nc.vector.tensor_copy(out=w1p[:], in_=w1raw[:].rearrange("p (m t) -> p t m", t=4))
+        nc.vector.quantize_mx(
+            out=cbc[:, 0:P].bitcast(FP8X4), scales=cbs[:, 0:P], in_=gc[:].rearrange("p r e -> p (r e)")
+        )
+        nc.vector.tensor_copy(out=s1p[:], in_=s1raw[:].rearrange("p (m t) -> p t m", t=4))
+        quant_a(ga0, 0, 1)
+
+        def spread_c(r0, r1):
+            nc.vector.tensor_copy(
+                out=crc[:, :, r0:r1, :],
+                in_=cbc[:, 0:P].rearrange("p (z w) -> p z w", z=Z).unsqueeze(2).to_broadcast([P, Z, r1 - r0, W]),
+            )
+            nc.vector.tensor_copy(
+                out=crs[:, :, r0:r1, :].bitcast(I32),
+                in_=cbs[:, 0:P].bitcast(I32).rearrange("p (z w) -> p z w", z=Z).unsqueeze(2).to_broadcast([P, Z, r1 - r0, W // 4]),
+            )
+
+        spread_c(0, 4)
+        nc.vector.quantize_mx(
+            out=cbc[:, P : 2 * P].bitcast(FP8X4), scales=cbs[:, P : 2 * P], in_=gb[:].rearrange("p r e -> p (r e)")
+        )
         for q in range(4):
             widen(1, q, False)
-        nc.vector.tensor_copy(out=w1p[:], in_=w1raw[:].rearrange("p (m t) -> p t m", t=4))
-        nc.vector.tensor_copy(out=s1p[:], in_=s1raw[:].rearrange("p (m t) -> p t m", t=4))
-        nc.vector.quantize_mx(
-            out=cbc[:].bitcast(FP8X4), scales=cbs[:], in_=gcb[:].rearrange("p s r e -> p (s r e)")
-        )
-        nc.vector.tensor_copy(
-            out=crc[:], in_=cbc[:, 0:P].rearrange("p (z w) -> p z w", z=Z).unsqueeze(2).to_broadcast([P, Z, 4, W])
-        )
-        nc.vector.tensor_copy(
-            out=crs[:].rearrange("p z a w -> p (z a w)").bitcast(I32).rearrange("p (z a w) -> p z a w", z=Z, a=4),
-            in_=cbs[:, 0:P].bitcast(I32).rearrange("p (z w) -> p z w", z=Z).unsqueeze(2).to_broadcast([P, Z, 4, W // 4]),
-        )
-        quant_a(ga0, 0, 1)
-        nc.vector.tensor_copy(out=b1f[:], in_=b1t[:])
-        nc.vector.tensor_scalar(out=gq[:], in0=gt[:], scalar1=1.0 / CLIP, scalar2=None, op0=ALU.mult)
+        late_b = cbs[:, P : 2 * P].rearrange("p (z h) -> p z h", z=Z)[:, :, 16:32]
+        for i in range(4):
+            nc.gpsimd.tensor_copy(out=bsq[:, :, :, i], in_=late_b)
+        for z in range(Z):
+            nc.gpsimd.tensor_copy(
+                out=brs[:, z].rearrange("p a w -> p (a w)").bitcast(I32).rearrange("p (a w) -> p a w", a=16),
+                in_=bsq[:, z].rearrange("p a i -> p (a i)").bitcast(I32).unsqueeze(2).to_broadcast([P, 16, W // 4]),
+            )
+            nc.gpsimd.tensor_copy(
+                out=brc[:, z],
+                in_=cbc[:, P + 32 * z + 16 : P + 32 * z + 32].unsqueeze(2).to_broadcast([P, 16, W]),
+            )
         bb = pmm.tile([P, 4, P], F32, name="mmb")
         for t in range(4):
             nc.tensor.matmul_mx(
@@ -289,40 +365,67 @@ def tile_tpvformersoftplusoccupancydecoder_d1p_kernel(
         )
         turn_a(1, 1)
         ga = copy_a(1)
-        for j in (2, 3):
+        for j in range(2, NU):
             for q in range(4):
                 widen(j, q, False)
 
-        for j in range(NU):
-            if j == 0:
-                quant_a(ga, 1, 1)
+        quant_a(ga, 1, 1)
+        gas = {}
+        for j in range(4):
             for z in range(Z):
                 bank = project(j, z)
                 add_b(j, z, bank)
-                if z % 2 == 1:
-                    expo(j, z // 2)
-            clip(j)
+            if j == 1:
+                spread_c(4, 16)
             if j < 3:
-                first = 2 * j + 2
-                turn_a(first, 2)
-                ga = copy_a(2)
-                quant_a(ga, first, 2)
-                if j < 2:
-                    for jj in (first + 2, first + 3):
-                        for q in range(4):
-                            widen(jj, q, False)
-            if j in (3, 5, 7):
-                guard(j // 2 - 1)
-        for j in range(NU):
+                turn_a(2 * j + 2, 2)
+                gas[j] = copy_a(2)
+            for half in range(2):
+                expo(j, half)
+            if j > 0:
+                quant_a(gas[j - 1], 2 * j, 2)
+        y_project(0)
+        y_evacuate(0)
+        clip(0)
+        clip(1)
+        guard(0)
+        clip(2)
+        clip(3)
+        guard(1)
+        y_project(1)
+        y_evacuate(1, False)
+        clip(4)
+        y_excess(1)
+        clip(5)
+        y_project(2)
+        for j in range(6):
             loga(j)
 
-        for k in range(NU + 2):
-            if k < NU:
-                combine(k)
-            if k == 0:
-                guard(3)
-            if 1 <= k <= NU:
-                quant_v(k - 1)
-                decode(k - 1)
+        def step(k):
+            combine(k)
             if k >= 2:
                 finish(k - 2)
+            if k >= 1:
+                quant_v(k - 1)
+                decode(k - 1)
+
+        for k in range(4):
+            step(k)
+        y_evacuate(2)
+        y_project(3)
+        y_evacuate(3)
+        step(4)
+        clip(6)
+        step(5)
+        clip(7)
+        loga(6)
+        loga(7)
+        step(6)
+        combine(7)
+        finish(5)
+        quant_v(6)
+        decode(6)
+        quant_v(7)
+        decode(7)
+        finish(6)
+        finish(7)

@@ -223,29 +223,19 @@ def tile_tpvformersoftplusoccupancydecoder_d1p_kernel(
                     )
                 ybanks[z, t] = bank
 
-        def y_evacuate(z, excess=True):
+        def y_evacuate(z):
             es[4 + z] = epool.tile([P, 4, 512], F32, name="et")
             ya[z] = apool.tile([P, 4, 512], F32, name="yt")
             for t in range(4):
                 bank = ybanks[z, t]
                 nc.scalar.activation(out=es[4 + z][:, t, :], in_=bank[:], func=AF.Exp, bias=b1f[:, t : t + 1])
-                if not excess:
-                    continue
                 nc.scalar.activation(out=ya[z][:, t, :], in_=bank[:], func=AF.Relu, bias=b1c[:, t : t + 1])
-                nc.gpsimd.tensor_scalar(
-                    out=ya[z][:, t, :], in0=ya[z][:, t, :],
-                    scalar1=gq[:, t : t + 1], scalar2=gf[:, t : t + 1], op0=ALU.mult, op1=ALU.add,
-                )
 
-        def y_excess(z):
+        def y_guard(z):
             for t in range(4):
+                a = ya[z][:, t, :]
                 nc.vector.tensor_scalar(
-                    out=ya[z][:, t, :], in0=ybanks[z, t][:], scalar1=b1c[:, t : t + 1], scalar2=0.0,
-                    op0=ALU.add, op1=ALU.max,
-                )
-                nc.gpsimd.tensor_scalar(
-                    out=ya[z][:, t, :], in0=ya[z][:, t, :],
-                    scalar1=gq[:, t : t + 1], scalar2=gf[:, t : t + 1], op0=ALU.mult, op1=ALU.add,
+                    out=a, in0=a, scalar1=gq[:, t : t + 1], scalar2=gf[:, t : t + 1], op0=ALU.mult, op1=ALU.add
                 )
 
         vts, vqs, obs = {}, {}, {}
@@ -299,7 +289,7 @@ def tile_tpvformersoftplusoccupancydecoder_d1p_kernel(
                 nc.sync.dma_start(out=dst, in_=ot[:])
 
         for q in range(4):
-            widen(0, q, True)
+            widen(0, q, q < 2)
         cbank = ptr.tile([P, 2, 2, P], F32, name="trb")
         turn(cbank[:, 0], xc[:])
         gc = grp.tile([P, P, 4], BF16, name="gc", align_bytes=64)
@@ -321,6 +311,9 @@ def tile_tpvformersoftplusoccupancydecoder_d1p_kernel(
             out=cbc[:, 0:P].bitcast(FP8X4), scales=cbs[:, 0:P], in_=gc[:].rearrange("p r e -> p (r e)")
         )
         nc.vector.tensor_copy(out=s1p[:], in_=s1raw[:].rearrange("p (m t) -> p t m", t=4))
+        nc.vector.quantize_mx(
+            out=cbc[:, P : 2 * P].bitcast(FP8X4), scales=cbs[:, P : 2 * P], in_=gb[:].rearrange("p r e -> p (r e)")
+        )
         quant_a(ga0, 0, 1)
 
         def spread_c(r0, r1):
@@ -334,23 +327,23 @@ def tile_tpvformersoftplusoccupancydecoder_d1p_kernel(
             )
 
         spread_c(0, 4)
-        nc.vector.quantize_mx(
-            out=cbc[:, P : 2 * P].bitcast(FP8X4), scales=cbs[:, P : 2 * P], in_=gb[:].rearrange("p r e -> p (r e)")
-        )
         for q in range(4):
             widen(1, q, False)
-        late_b = cbs[:, P : 2 * P].rearrange("p (z h) -> p z h", z=Z)[:, :, 16:32]
-        for i in range(4):
-            nc.gpsimd.tensor_copy(out=bsq[:, :, :, i], in_=late_b)
-        for z in range(Z):
-            nc.gpsimd.tensor_copy(
-                out=brs[:, z].rearrange("p a w -> p (a w)").bitcast(I32).rearrange("p (a w) -> p a w", a=16),
-                in_=bsq[:, z].rearrange("p a i -> p (a i)").bitcast(I32).unsqueeze(2).to_broadcast([P, 16, W // 4]),
+        def spread_b_scales():
+            late = cbs[:, P : 2 * P].rearrange("p (z h) -> p z h", z=Z)[:, :, 16:32]
+            for i in range(4):
+                nc.vector.tensor_copy(out=bsq[:, :, :, i], in_=late)
+            nc.vector.tensor_copy(
+                out=brs[:].rearrange("p z a w -> p (z a w)").bitcast(I32).rearrange("p (r w) -> p r w", w=W // 4),
+                in_=bsq[:].rearrange("p z a i -> p (z a i)").bitcast(I32).unsqueeze(2).to_broadcast([P, 16 * Z, W // 4]),
             )
-            nc.gpsimd.tensor_copy(
+
+        def spread_b(z):
+            nc.vector.tensor_copy(
                 out=brc[:, z],
                 in_=cbc[:, P + 32 * z + 16 : P + 32 * z + 32].unsqueeze(2).to_broadcast([P, 16, W]),
             )
+
         bb = pmm.tile([P, 4, P], F32, name="mmb")
         for t in range(4):
             nc.tensor.matmul_mx(
@@ -363,18 +356,18 @@ def tile_tpvformersoftplusoccupancydecoder_d1p_kernel(
             out=bp[:].rearrange("p t z h -> p t (z h)"), in0=bb[:],
             in1=b1f[:].unsqueeze(2).to_broadcast([P, 4, P]), op=ALU.add,
         )
-        turn_a(1, 1)
-        ga = copy_a(1)
         for j in range(2, NU):
             for q in range(4):
                 widen(j, q, False)
 
-        quant_a(ga, 1, 1)
         gas = {}
         for j in range(4):
             for z in range(Z):
                 bank = project(j, z)
                 add_b(j, z, bank)
+            if j == 0:
+                turn_a(1, 1)
+                quant_a(copy_a(1), 1, 1)
             if j == 1:
                 spread_c(4, 16)
             if j < 3:
@@ -384,18 +377,26 @@ def tile_tpvformersoftplusoccupancydecoder_d1p_kernel(
                 expo(j, half)
             if j > 0:
                 quant_a(gas[j - 1], 2 * j, 2)
+            if j == 1:
+                spread_b_scales()
+                spread_b(0)
+            if j == 2:
+                spread_b(1)
         y_project(0)
         y_evacuate(0)
         clip(0)
+        spread_b(2)
+        spread_b(3)
         clip(1)
         guard(0)
         clip(2)
         clip(3)
         guard(1)
         y_project(1)
-        y_evacuate(1, False)
+        y_evacuate(1)
+        y_guard(0)
         clip(4)
-        y_excess(1)
+        y_guard(1)
         clip(5)
         y_project(2)
         for j in range(6):
@@ -415,16 +416,18 @@ def tile_tpvformersoftplusoccupancydecoder_d1p_kernel(
         y_project(3)
         y_evacuate(3)
         step(4)
+        y_guard(2)
         clip(6)
         step(5)
+        y_guard(3)
         clip(7)
         loga(6)
         loga(7)
         step(6)
         combine(7)
-        finish(5)
         quant_v(6)
         decode(6)
+        finish(5)
         quant_v(7)
         decode(7)
         finish(6)

import math
from contextlib import ExitStack

import concourse.mybir as mybir
from concourse.masks import make_identity

H, W, Z, D, F, E = 32, 32, 4, 512, 512, 256
FLOPS = 2 * (H * W + Z * H + W * Z) * D * F + 2 * H * W * Z * F * E

F32 = mybir.dt.float32
BF16 = mybir.dt.bfloat16
I32 = mybir.dt.int32
U32 = mybir.dt.uint32
U8 = mybir.dt.uint8
FP8 = mybir.dt.float8_e4m3fn
FP8X4 = mybir.dt.float8_e4m3fn_x4
AF = mybir.ActivationFunctionType
ALU = mybir.AluOpType

P = 128
NU = 8
CLIP = 32.0
ECLIP = math.exp(CLIP)


def tile_tpvformersoftplusoccupancydecoder_d1p_kernel(
    tc, thw_bytes, thw_scale, tzh, twz, w1_words, w1_scales, b1, g, w2_words, w2_scales, b2, out
):
    nc = tc.nc
    with ExitStack() as ctx:
        keep = ctx.enter_context(tc.tile_pool(name="keep", bufs=1))
        head = ctx.enter_context(tc.tile_pool(name="head", bufs=1))
        grp = ctx.enter_context(tc.tile_pool(name="grp", bufs=2))
        upool = ctx.enter_context(tc.tile_pool(name="upool", bufs=2))
        apool = ctx.enter_context(tc.tile_pool(name="apool", bufs=4))
        epool = ctx.enter_context(tc.tile_pool(name="epool", bufs=8))
        vpool = ctx.enter_context(tc.tile_pool(name="vpool", bufs=3))
        opool = ctx.enter_context(tc.tile_pool(name="opool", bufs=3))
        ptr = ctx.enter_context(tc.psum_pool(name="ptr", bufs=2))
        pmm = ctx.enter_context(tc.psum_pool(name="pmm", bufs=4))
        pout = ctx.enter_context(tc.psum_pool(name="pout", bufs=2))
        ctx.enter_context(tc.manual_schedule())

        ident = keep.tile([P, P], F32)
        byt = keep.tile([P, NU, D], U8)
        sc0 = keep.tile([P, 4], F32)
        sc = keep.tile([P, NU - 1, 4], F32)
        xa = keep.tile([P, NU, D], BF16, align_bytes=64)
        xc = keep.tile([P, D], BF16, align_bytes=64)
        xb = keep.tile([P, D], BF16, align_bytes=64)
        w1raw = head.tile([P, F], I32, align_bytes=64)
        s1raw = head.tile([P, F], U8, align_bytes=64)
        w1p = keep.tile([P, 4, P], I32, align_bytes=64)
        s1p = keep.tile([P, 4, P], U8, align_bytes=64)
        w2w = keep.tile([P, E], I32, align_bytes=64)
        s2w = keep.tile([P, E], U8, align_bytes=64)
        b1t = keep.tile([P, 4], BF16)
        gt = keep.tile([P, 4], BF16)
        b1f = keep.tile([P, 4], F32)
        gq = keep.tile([P, 4], F32)
        b2t = keep.tile([P, E], BF16)
        cbc = keep.tile([P, 2 * P], I32, align_bytes=64)
        cbs = keep.tile([P, 2 * P], U8, align_bytes=64)
        crc = keep.tile([P, Z, 16, W], I32, align_bytes=64)
        crs = keep.tile([P, Z, 16, W], U8, align_bytes=64)
        brc = keep.tile([P, Z, 16, W], I32, align_bytes=64)
        brs = keep.tile([P, Z, 16, W], U8, align_bytes=64)
        bsq = keep.tile([P, Z, 16, 4], U8, align_bytes=64)
        gf = keep.tile([P, 4], F32)
        b1c = keep.tile([P, 4], F32)
        ac = keep.tile([P, NU, P], U32, align_bytes=64)
        as_ = keep.tile([P, NU, P], U8, align_bytes=64)
        bp = keep.tile([P, 4, Z, H], F32)
        dum = keep.tile([P, 1], F32)

        bytes_v = thw_bytes.rearrange("(j a) w k -> (a w) j k", a=4)
        scale_v = thw_scale.rearrange("(j a) w q -> (a w) j q", a=4)
        nc.vector.memset(dum[:], 0.0)
        nc.vector.memset(s1raw[:].bitcast(I32), 0)
        nc.vector.memset(cbs[:].bitcast(I32), 0)
        nc.vector.memset(s2w[:].bitcast(I32), 0)

        def load_s1(q, eng):
            eng.dma_start(
                out=s1raw[32 * q : 32 * q + 4, :].bitcast(I32),
                in_=w1_scales[0, 4 * q : 4 * q + 4, :].bitcast(I32),
            )

        nc.sync.dma_start(out=byt[:, 0, :], in_=bytes_v[:, 0, :])
        nc.scalar.dma_start(out=sc0[:], in_=scale_v[:, 0, :])
        nc.sync.dma_start(out=xc[:], in_=twz.rearrange("w z d -> (w z) d"))
        nc.scalar.dma_start(out=w1raw[:], in_=w1_words[0].rearrange("p n t -> p (n t)").bitcast(I32))
        nc.sync.dma_start(out=xb[:], in_=tzh.rearrange("z h d -> (z h) d"))
        load_s1(0, nc.scalar)
        load_s1(1, nc.scalar)
        load_s1(2, nc.sync)
        load_s1(3, nc.sync)
        nc.scalar.activation(out=dum[:], in_=dum[:], func=AF.Exp)
        nc.sync.dma_start(out=b1t[:], in_=b1.rearrange("(p t) -> p t", t=4))
        nc.sync.dma_start(out=byt[:, 1, :], in_=bytes_v[:, 1, :])
        nc.sync.dma_start(out=sc[:], in_=scale_v[:, 1:, :])
        nc.sync.dma_start(out=byt[:, 2:4, :], in_=bytes_v[:, 2:4, :])
        make_identity(nc, ident[:])
        nc.gpsimd.dma_start(out=gt[:], in_=g.rearrange("(p t) -> p t", t=4))
        nc.sync.dma_start(out=byt[:, 4:8, :], in_=bytes_v[:, 4:8, :])
        nc.sync.dma_start(out=w2w[:], in_=w2_words[0].rearrange("p n t -> p (n t)").bitcast(I32))
        for q in range(4):
            nc.sync.dma_start(
                out=s2w[32 * q : 32 * q + 4, :].bitcast(I32),
                in_=w2_scales[0, 4 * q : 4 * q + 4, :].bitcast(I32),
            )
        nc.sync.dma_start(out=b2t[:], in_=b2.partition_broadcast(P))
        nc.gpsimd.tensor_copy(out=b1f[:], in_=b1t[:])
        nc.gpsimd.tensor_scalar(out=gq[:], in0=gt[:], scalar1=1.0 / CLIP, scalar2=0.0, op0=ALU.mult, op1=ALU.add)
        nc.gpsimd.tensor_copy(out=gf[:], in_=gt[:])
        nc.gpsimd.tensor_scalar(out=b1c[:], in0=b1t[:], scalar1=1.0, scalar2=-CLIP, op0=ALU.mult, op1=ALU.add)

        def widen(j, q, vec):
            cols = slice(128 * q, 128 * q + 128)
            src = byt[:, j, cols].bitcast(FP8)
            s = sc0[:, q : q + 1] if j == 0 else sc[:, j - 1, q : q + 1]
            if vec:
                nc.vector.tensor_scalar(out=xa[:, j, cols], in0=src, scalar1=s, scalar2=None, op0=ALU.mult)
            else:
                nc.scalar.activation(out=xa[:, j, cols], in_=src, func=AF.Copy, scale=s)

        def turn(dst, src):
            words = src.bitcast(F32)
            for u in range(2):
                nc.tensor.transpose(dst[:, u, :], words[:, u : 2 * P : 2], ident[:])

        banks = {}

        def turn_a(first, count):
            bank = ptr.tile([P, 2, 2, P], F32, name="trb")
            for s in range(count):
                turn(bank[:, s], xa[:, first + s, :])
            banks["a"] = bank

        def copy_a(count):
            ga = grp.tile([P, 2, P, 4], BF16, name="ga", align_bytes=64)
            nc.scalar.copy(
                out=ga[:, 0:count].rearrange("p s r e -> p (s r e)").bitcast(F32).rearrange("p (s r u) -> p s r u", s=count, u=2),
                in_=banks["a"][:, 0:count].rearrange("p s u r -> p s r u"),
            )
            return ga

        def quant_a(ga, first, count):
            nc.vector.quantize_mx(
                out=ac[:, first : first + count, :].rearrange("p s r -> p (s r)").bitcast(FP8X4),
                scales=as_[:, first : first + count, :].rearrange("p s r -> p (s r)"),
                in_=ga[:, 0:count].rearrange("p s r e -> p (s r e)"),
            )

        def project(j, z):
            bank = pmm.tile([P, 4, P], F32, name="mmb")
            for t in range(4):
                nc.tensor.matmul_mx(
                    out=bank[:, t, :],
                    lhsT=w1p[:, t, :].bitcast(FP8X4), lhsT_scale=s1p[:, t, :],
                    rhs=ac[:, j, :].bitcast(FP8X4), rhs_scale=as_[:, j, :],
                    start=True, stop=False,
                )
                nc.tensor.matmul_mx(
                    out=bank[:, t, :],
                    lhsT=w1p[:, t, :].bitcast(FP8X4), lhsT_scale=s1p[:, t, :],
                    rhs=crc[:, z, 0:4].rearrange("p a w -> p (a w)").bitcast(FP8X4),
                    rhs_scale=crs[:, z, 0:4].rearrange("p a w -> p (a w)"),
                    start=False, stop=True,
                )
            return bank

        us, es = {}, {}

        def add_b(j, z, bank):
            pair, s = divmod(j, 2)
            if s == 0 and z == 0:
                us[pair] = upool.tile([P, 4, 2, 512], F32, name="ut")
            nc.vector.tensor_tensor(
                out=us[pair][:, :, s, 128 * z : 128 * z + 128].rearrange("p t (a w) -> p t a w", a=4),
                in0=bank[:].rearrange("p t (a w) -> p t a w", a=4),
                in1=bp[:, :, z, 4 * j : 4 * j + 4].unsqueeze(3).to_broadcast([P, 4, 4, W]),
                op=ALU.add,
            )

        def expo(j, half):
            pair, s = divmod(j, 2)
            if half == 0:
                es[j] = epool.tile([P, 4, 512], F32, name="et")
            cols = slice(256 * half, 256 * half + 256)
            nc.scalar.activation(out=es[j][:, :, cols], in_=us[pair][:, :, s, cols], func=AF.Exp)

        def clip(j):
            e = es[j][:].rearrange("p t n -> p (t n)")
            nc.vector.tensor_scalar(out=e, in0=e, scalar1=ECLIP, scalar2=None, op0=ALU.min)

        def loga(j):
            e = es[j][:].rearrange("p t n -> p (t n)")
            nc.scalar.activation(out=e, in_=e, func=AF.Ln, bias=1.0)

        def guard(pair):
            for t in range(4):
                a = us[pair][:, t].rearrange("p s n -> p (s n)")
                nc.vector.tensor_scalar(
                    out=a, in0=a, scalar1=CLIP, scalar2=gq[:, t : t + 1], op0=ALU.max, op1=ALU.mult
                )

        ybanks, ya = {}, {}

        def y_project(z):
            for t in range(4):
                bank = pmm.tile([P, 512], F32, name="mmb")
                for i, (codes, scales) in enumerate((
                    (ac[:, 4:8].rearrange("p j r -> p (j r)"), as_[:, 4:8].rearrange("p j r -> p (j r)")),
                    (crc[:, z].rearrange("p a w -> p (a w)"), crs[:, z].rearrange("p a w -> p (a w)")),
                    (brc[:, z].rearrange("p a w -> p (a w)"), brs[:, z].rearrange("p a w -> p (a w)")),
                )):
                    nc.tensor.matmul_mx(
                        out=bank[:],
                        lhsT=w1p[:, t, :].bitcast(FP8X4), lhsT_scale=s1p[:, t, :],
                        rhs=codes.bitcast(FP8X4), rhs_scale=scales,
                        start=i == 0, stop=i == 2,
                    )
                ybanks[z, t] = bank

        def y_evacuate(z):
            es[4 + z] = epool.tile([P, 4, 512], F32, name="et")
            ya[z] = apool.tile([P, 4, 512], F32, name="yt")
            for t in range(4):
                bank = ybanks[z, t]
                nc.scalar.activation(out=es[4 + z][:, t, :], in_=bank[:], func=AF.Exp, bias=b1f[:, t : t + 1])
                nc.scalar.activation(out=ya[z][:, t, :], in_=bank[:], func=AF.Relu, bias=b1c[:, t : t + 1])

        def y_guard(z):
            for t in range(4):
                a = ya[z][:, t, :]
                nc.vector.tensor_scalar(
                    out=a, in0=a, scalar1=gq[:, t : t + 1], scalar2=gf[:, t : t + 1], op0=ALU.mult, op1=ALU.add
                )

        vts, vqs, obs = {}, {}, {}

        def combine(j):
            a = us[j // 2][:, :, j % 2, :] if j < 4 else ya[j - 4][:]
            vt = vpool.tile([P, 512, 4], BF16, name="vt", align_bytes=64)
            nc.vector.tensor_tensor(
                out=vt[:].rearrange("p (c i) t -> p c t i", i=4),
                in0=es[j][:].rearrange("p t (c i) -> p c t i", i=4),
                in1=a.rearrange("p t (c i) -> p c t i", i=4),
                op=ALU.mult,
            )
            vts[j] = vt

        def quant_v(j):
            vc = vpool.tile([P, 512], U32, name="vc", align_bytes=64)
            vs = vpool.tile([P, 512], U8, name="vs", align_bytes=64)
            nc.vector.quantize_mx(
                out=vc[:].bitcast(FP8X4), scales=vs[:], in_=vts[j][:].rearrange("p n t -> p (n t)")
            )
            vqs[j] = (vc, vs)

        def decode(j):
            vc, vs = vqs[j]
            for zp in range(2):
                ob = pout.tile([P, 2, E], F32, name="ob")
                for zz in range(2):
                    cols = slice(128 * (2 * zp + zz), 128 * (2 * zp + zz) + 128)
                    nc.tensor.matmul_mx(
                        out=ob[:, zz, :],
                        lhsT=vc[:, cols].bitcast(FP8X4), lhsT_scale=vs[:, cols],
                        rhs=w2w[:].bitcast(FP8X4), rhs_scale=s2w[:],
                        start=True, stop=True,
                    )
                obs[j, zp] = ob

        out_v = out.rearrange("(j a) w z e -> (a w) j z e", a=4)

        def finish(j):
            ot = opool.tile([P, 4, E], F32, name="ot")
            dst = out_v[:, j] if j < 4 else out_v[:, 4:8, j - 4, :]
            for zp in range(2):
                nc.vector.tensor_tensor(
                    out=ot[:, 2 * zp : 2 * zp + 2, :], in0=obs[j, zp][:],
                    in1=b2t[:].unsqueeze(1).to_broadcast([P, 2, E]), op=ALU.add,
                )
                if j == NU - 1:
                    nc.sync.dma_start(out=dst[:, 2 * zp : 2 * zp + 2], in_=ot[:, 2 * zp : 2 * zp + 2, :])
            if j < NU - 1:
                nc.sync.dma_start(out=dst, in_=ot[:])

        for q in range(4):
            widen(0, q, q < 2)
        cbank = ptr.tile([P, 2, 2, P], F32, name="trb")
        turn(cbank[:, 0], xc[:])
        gc = grp.tile([P, P, 4], BF16, name="gc", align_bytes=64)
        nc.vector.tensor_copy(
            out=gc[:].rearrange("p r e -> p (r e)").bitcast(F32).rearrange("p (z w u) -> p z w u", z=Z, u=2),
            in_=cbank[:, 0].rearrange("p u (w z) -> p z w u", z=Z),
        )
        turn_a(0, 1)
        ga0 = copy_a(1)
        bbank = ptr.tile([P, 2, 2, P], F32, name="trb")
        turn(bbank[:, 0], xb[:])
        gb = grp.tile([P, P, 4], BF16, name="gb", align_bytes=64)
        nc.scalar.copy(
            out=gb[:].rearrange("p r e -> p (r e)").bitcast(F32).rearrange("p (r u) -> p r u", u=2),
            in_=bbank[:, 0].rearrange("p u r -> p r u"),
        )
        nc.vector.tensor_copy(out=w1p[:], in_=w1raw[:].rearrange("p (m t) -> p t m", t=4))
        nc.vector.quantize_mx(
            out=cbc[:, 0:P].bitcast(FP8X4), scales=cbs[:, 0:P], in_=gc[:].rearrange("p r e -> p (r e)")
        )
        nc.vector.tensor_copy(out=s1p[:], in_=s1raw[:].rearrange("p (m t) -> p t m", t=4))
        nc.vector.quantize_mx(
            out=cbc[:, P : 2 * P].bitcast(FP8X4), scales=cbs[:, P : 2 * P], in_=gb[:].rearrange("p r e -> p (r e)")
        )
        quant_a(ga0, 0, 1)

        def spread_c(r0, r1):
            nc.vector.tensor_copy(
                out=crc[:, :, r0:r1, :],
                in_=cbc[:, 0:P].rearrange("p (z w) -> p z w", z=Z).unsqueeze(2).to_broadcast([P, Z, r1 - r0, W]),
            )
            nc.vector.tensor_copy(
                out=crs[:, :, r0:r1, :].bitcast(I32),
                in_=cbs[:, 0:P].bitcast(I32).rearrange("p (z w) -> p z w", z=Z).unsqueeze(2).to_broadcast([P, Z, r1 - r0, W // 4]),
            )

        spread_c(0, 4)
        for q in range(4):
            widen(1, q, False)
        def spread_b_scales():
            late = cbs[:, P : 2 * P].rearrange("p (z h) -> p z h", z=Z)[:, :, 16:32]
            for i in range(4):
                nc.vector.tensor_copy(out=bsq[:, :, :, i], in_=late)
            nc.vector.tensor_copy(
                out=brs[:].rearrange("p z a w -> p (z a w)").bitcast(I32).rearrange("p (r w) -> p r w", w=W // 4),
                in_=bsq[:].rearrange("p z a i -> p (z a i)").bitcast(I32).unsqueeze(2).to_broadcast([P, 16 * Z, W // 4]),
            )

        def spread_b(z):
            nc.vector.tensor_copy(
                out=brc[:, z],
                in_=cbc[:, P + 32 * z + 16 : P + 32 * z + 32].unsqueeze(2).to_broadcast([P, 16, W]),
            )

        bb = pmm.tile([P, 4, P], F32, name="mmb")
        for t in range(4):
            nc.tensor.matmul_mx(
                out=bb[:, t, :],
                lhsT=w1p[:, t, :].bitcast(FP8X4), lhsT_scale=s1p[:, t, :],
                rhs=cbc[:, P : 2 * P].bitcast(FP8X4), rhs_scale=cbs[:, P : 2 * P],
                start=True, stop=True,
            )
        nc.vector.tensor_tensor(
            out=bp[:].rearrange("p t z h -> p t (z h)"), in0=bb[:],
            in1=b1f[:].unsqueeze(2).to_broadcast([P, 4, P]), op=ALU.add,
        )
        for j in range(2, NU):
            for q in range(4):
                widen(j, q, False)

        gas = {}
        for j in range(4):
            for z in range(Z):
                bank = project(j, z)
                add_b(j, z, bank)
            if j == 0:
                turn_a(1, 1)
                quant_a(copy_a(1), 1, 1)
            if j == 1:
                spread_c(4, 16)
            if j < 3:
                turn_a(2 * j + 2, 2)
                gas[j] = copy_a(2)
            for half in range(2):
                expo(j, half)
            if j > 0:
                quant_a(gas[j - 1], 2 * j, 2)
            if j == 1:
                spread_b_scales()
                spread_b(0)
            if j == 2:
                spread_b(1)
        y_project(0)
        y_evacuate(0)
        clip(0)
        spread_b(2)
        spread_b(3)
        clip(1)
        guard(0)
        clip(2)
        clip(3)
        guard(1)
        y_project(1)
        y_evacuate(1)
        y_guard(0)
        clip(4)
        y_guard(1)
        clip(5)
        y_project(2)
        for j in range(6):
            loga(j)

        def step(k):
            combine(k)
            if k >= 2:
                finish(k - 2)
            if k >= 1:
                quant_v(k - 1)
                decode(k - 1)

        for k in range(4):
            step(k)
        y_evacuate(2)
        y_project(3)
        y_evacuate(3)
        step(4)
        y_guard(2)
        clip(6)
        step(5)
        y_guard(3)
        clip(7)
        loga(6)
        loga(7)
        step(6)
        combine(7)
        quant_v(6)
        decode(6)
        finish(5)
        quant_v(7)
        decode(7)
        finish(6)
        finish(7)
